import numpy as np
import ml_dtypes


def mxq(x, axis, fmt="e4m3"):
    dtype, down = {"e4m3": (ml_dtypes.float8_e4m3fn, 7), "e5m2": (ml_dtypes.float8_e5m2, 14)}[fmt]
    v = np.moveaxis(np.asarray(x, np.float32).astype(ml_dtypes.bfloat16).astype(np.float64), axis, -1)
    blocks = v.reshape(v.shape[:-1] + (-1, 32))
    amax = np.abs(blocks).max(-1, keepdims=True)
    byte = np.maximum(np.where(amax > 0, np.frexp(amax)[1] - 1 + 127, 0) - down, 1)
    scale = np.exp2(byte - 127.0)
    codes = (blocks / scale).astype(np.float32).astype(dtype).astype(np.float64)
    return np.moveaxis((codes * scale).reshape(v.shape), -1, axis)


WIDE = False


def mx_kscale(k):
    if not WIDE:
        return np.ones(k)
    levels = np.array([10, -10, 5, -5, 0])
    if k % 512:
        return np.exp2(np.random.permutation(np.resize(levels, k // 32))).repeat(32)
    a = np.empty((k // 512, 16))
    for p in range(k // 512):
        a[p, :8] = np.random.permutation(np.resize(levels, 8))
        for g in range(8):
            far = levels[np.abs(levels - a[p, g]) >= 10]
            a[p, g + 8] = far[np.random.randint(len(far))]
    return np.exp2(a.ravel()).repeat(32)


def f64(x):
    return np.asarray(x).astype(np.float64)


def striped(idx):
    return np.tile(np.asarray(idx).reshape(-1, 16).T, (8, 1)).astype(np.uint16)


def unstriped(offs):
    return offs[:16].T.reshape(-1).astype(np.int64)


E2M1 = np.array([0.0, 0.5, 1.0, 1.5, 2.0, 3.0, 4.0, 6.0, -0.0, -0.5, -1.0, -1.5, -2.0, -3.0, -4.0, -6.0])


def pack_weight(w, fmt):
    k, n = w.shape
    w = f64(np.asarray(w, np.float32).astype(ml_dtypes.bfloat16)).reshape(k // 32, 32, n)
    amax = np.abs(w).max(1)
    if fmt == "e4m3":
        byte = np.frexp(amax)[1] - 1 + 127 - 7
    else:
        mant, ex = np.frexp(amax / 6.0)
        byte = np.where(mant > 0.5, ex, ex - 1) + 127
    byte = np.clip(np.where(amax > 0, byte, 1), 1, 254)
    scaled = (w * np.exp2(127.0 - byte)[:, None, :]).reshape(k, n).astype(np.float32)
    by_word = np.ascontiguousarray(scaled.reshape(k // 512, 128, 4, n).transpose(0, 1, 3, 2))
    if fmt == "e4m3":
        words = by_word.astype(ml_dtypes.float8_e4m3fn).view(np.uint8)
    else:
        c = by_word.astype(ml_dtypes.float4_e2m1fn).view(np.uint8) & 0xF
        words = (c[..., 0::2] | (c[..., 1::2] << 4)).reshape(k // 512, 128, 2 * n)
    return np.ascontiguousarray(words), np.ascontiguousarray(byte.astype(np.uint8).reshape(k // 512, 16, n))


def unpack_weight(words, scales, fmt):
    g, _, n = scales.shape
    words = np.ascontiguousarray(words).reshape(g, 128, n, -1)
    if fmt == "e4m3":
        vals = words.view(ml_dtypes.float8_e4m3fn).astype(np.float64)
    else:
        nib = np.empty((g, 128, n, 4), np.uint8)
        nib[..., 0::2] = words & 0xF
        nib[..., 1::2] = words >> 4
        vals = E2M1[nib]
    vals = vals * np.repeat(np.exp2(scales.astype(np.float64) - 127.0), 8, axis=1)[..., None]
    return vals.transpose(0, 1, 3, 2).reshape(g * 512, n)


def softplus(v):
    return np.log(1.0 + np.exp(v))


D, K, R, T, I, Q, G = 512, 512, 512, 2048, 512, 128, 64


def setup_inputs():
    n = np.random.standard_normal
    idx = np.random.permutation(T)[:I]
    fd = mx_kscale(D)
    fk = mx_kscale(K)
    fi = mx_kscale(I)
    keysp = pack_weight(n((D, T)) / fd[:, None], "e4m3")
    tabp = pack_weight(n((K, T)) / fk[:, None], "e4m3")
    return {
        "query": (n((D, Q)) * 0.9 / np.sqrt(D) * fd[:, None]).astype(np.float32),
        "keys_words": keysp[0],
        "keys_scales": keysp[1],
        "th": (np.random.uniform(-0.3, 0.6, (Q, 1))).astype(np.float32),
        "reserve": (np.random.uniform(50.0, 200.0, (Q, 1))).astype(np.float32),
        "tab_words": tabp[0],
        "tab_scales": tabp[1],
        "w1": (n((K, R)) * 1 / np.sqrt(K) * fk[:, None]).astype(np.float32),
        "temper": (np.random.uniform(0.4, 1.0, (R, 1))).astype(np.float32),
        "os": (np.random.uniform(4.0, 16.0, (1, I)) * fi).astype(np.float32),
        "vs": (np.random.uniform(0.5, 2.0, (1, I)) / fi).astype(np.float32),
        "offs": striped(idx),
    }


def reference(query, keys_words, keys_scales, th, reserve, tab_words, tab_scales, w1, temper, os, vs, offs):
    idx = unstriped(offs)
    keysu = unpack_weight(keys_words, keys_scales, "e4m3")
    tabu = unpack_weight(tab_words, tab_scales, "e4m3")
    queryq = mxq(f64(query), 0, "e4m3")
    keysidxg = keysu[:, idx]
    a = queryq.T @ keysidxg
    p = softplus(a - f64(th))
    z = np.sum(p, axis=1, keepdims=True) + f64(reserve)
    w = p / z
    w1q = mxq(f64(w1), 0, "e4m3")
    tabidxg = tabu[:, idx]
    zh = w1q.T @ tabidxg
    ht = np.exp(zh * f64(temper))
    mz = ht.reshape(R, G, I // G).sum(axis=2)
    mzr = np.repeat(mz, I // G, axis=1)
    hv = ht / mzr * 4.0
    wo1 = w * f64(os)
    wt1 = wo1.T
    hw = hv * f64(vs)
    ht1 = hw.T
    wt1q = mxq(wt1, 0, "e4m3")
    ht1q = mxq(ht1, 0, "e4m3")
    o = wt1q.T @ ht1q
    return o

@@ -1,0 +1,229 @@
+from contextlib import ExitStack
+
+import concourse.mybir as mybir
+from concourse.masks import make_identity
+
+F32 = mybir.dt.float32
+BF16 = mybir.dt.bfloat16
+I32 = mybir.dt.int32
+U32 = mybir.dt.uint32
+U16 = mybir.dt.uint16
+U8 = mybir.dt.uint8
+FP8X4 = mybir.dt.float8_e4m3fn_x4
+ACT = mybir.ActivationFunctionType
+ALU = mybir.AluOpType
+AXIS = mybir.AxisListType
+
+P = 128
+PACK = 4
+POOL = 2048
+SLOTS = 512
+HIDDEN = 512
+GROUPS = 64
+BLOCKS = HIDDEN // P
+FLOPS = 2 * 512 * 128 * 512 + 2 * 512 * 512 * 512 + 2 * 512 * 128 * 512
+
+
+def walk_planes(ap):
+    return ap.rearrange("p t (c i) -> p c t i", i=4)
+
+
+def walk_words(ap):
+    return ap.rearrange("p (c i) t -> p c t i", i=4)
+
+
+def tile_attend_lrshared_capped_kernel(
+    tc, query, keys_words, keys_scales, th, reserve, tab_words, tab_scales, w1, temper, slot_factor, value_scale, offs, out
+):
+    nc = tc.nc
+    with ExitStack() as ctx:
+        lists = ctx.enter_context(tc.tile_pool(name="lists", bufs=1))
+        keep = ctx.enter_context(tc.tile_pool(name="keep", bufs=1))
+        psum = ctx.enter_context(tc.psum_pool(name="psum", bufs=1))
+
+        offsets = lists.tile([P, SLOTS // 16], U16, name="offsets")
+        nc.sync.dma_start(offsets[:], offs)
+
+        def load_scales(queue, name, scales):
+            window = keep.tile([P, POOL], U8, name=name, align_bytes=64)
+            nc.vector.memset(window[:].bitcast(I32), 0)
+            for quad in range(4):
+                queue.dma_start(
+                    window[32 * quad : 32 * quad + 4, :].bitcast(I32), scales[0, 4 * quad : 4 * quad + 4, :].bitcast(I32)
+                )
+            return window
+
+        def load_words(name, words):
+            window = keep.tile([P, POOL], U32, name=name, tag=name, align_bytes=64)
+            nc.sync.dma_start(window[:].bitcast(I32), words[0].rearrange("p n t -> p (n t)").bitcast(I32))
+            return window
+
+        def gather(name, window, dtype):
+            picked = keep.tile([P, SLOTS], dtype, name=name, align_bytes=64)
+            nc.vector.tensor_copy(picked[:], window[:].indirect(offsets[:]))
+            return picked
+
+        def quantise(name, grouped):
+            codes = keep.tile([P, P], U32, name=name + "_codes", align_bytes=64)
+            scales = keep.tile([P, P], U8, name=name + "_scales", align_bytes=64)
+            nc.vector.quantize_mx(out=codes[:].bitcast(FP8X4), scales=scales[:], in_=grouped[:].rearrange("p c t -> p (c t)"))
+            return codes, scales
+
+        def product(acc, stationary, moving):
+            nc.tensor.matmul_mx(
+                out=acc,
+                lhsT=stationary[0][:].bitcast(FP8X4),
+                lhsT_scale=stationary[1][:],
+                rhs=moving[0][:].bitcast(FP8X4),
+                rhs_scale=moving[1][:],
+                start=True,
+                stop=True,
+            )
+
+        w1_rows = w1.rearrange("(p j) r -> p j r", j=PACK)
+        w1_raw = [keep.tile([P, PACK, 2 * P], F32, name="w1_raw%d" % half, tag="w1_raw%d" % half) for half in range(2)]
+        temper_sb = keep.tile([P, BLOCKS], F32, name="temper_sb")
+        with nc.allow_non_contiguous_dma(reason="one temper value a partition and block"):
+            nc.scalar.dma_start(temper_sb[:], temper.rearrange("(b p) o -> p (b o)", p=P))
+        nc.sync.dma_start(w1_raw[0][:], w1_rows[:, :, 0 : 2 * P])
+        tab_scale_window = load_scales(nc.sync, "tab_scale_window", tab_scales)
+        tab_window = load_words("tab_window", tab_words)
+        nc.sync.dma_start(w1_raw[1][:], w1_rows[:, :, 2 * P : 4 * P])
+        query_raw = keep.tile([P, PACK, P], F32, name="query_raw", tag="query_raw")
+        nc.sync.dma_start(query_raw[:], query.rearrange("(p j) q -> p j q", j=PACK))
+        keys_scale_window = load_scales(nc.sync, "keys_scale_window", keys_scales)
+        keys_window = load_words("keys_window", keys_words)
+        vs_sb = keep.tile([P, PACK], F32, name="vs_sb")
+        nc.sync.dma_start(vs_sb[:], value_scale.rearrange("o (p t) -> (o p) t", t=PACK))
+        th_sb = keep.tile([P, 1], F32, name="th_sb")
+        nc.sync.dma_start(th_sb[:], th)
+        os_sb = keep.tile([P, PACK], F32, name="os_sb")
+        nc.sync.dma_start(os_sb[:], slot_factor.rearrange("o (p t) -> (o p) t", t=PACK))
+        reserve_sb = keep.tile([P, 1], F32, name="reserve_sb")
+        nc.sync.dma_start(reserve_sb[:], reserve)
+
+        identity = keep.tile([P, P], F32, name="identity")
+        make_identity(nc, identity[:])
+        spaced = [keep.tile([P, 2 * GROUPS + 8], F32, name="spaced%d" % b) for b in range(BLOCKS)]
+        for b in range(BLOCKS):
+            nc.gpsimd.memset(spaced[b][:], 0.0)
+        vs4 = keep.tile([P, PACK], F32, name="vs4")
+        nc.gpsimd.tensor_scalar(vs4[:], vs_sb[:], 4.0, 0.0, ALU.mult, ALU.add)
+        minus_th = keep.tile([P, 1], F32, name="minus_th")
+        nc.gpsimd.tensor_scalar(minus_th[:], th_sb[:], -1.0, 0.0, ALU.mult, ALU.add)
+
+        tab_scale_picked = gather("tab_scale_picked", tab_scale_window, U8)
+
+        w1_q = []
+
+        def quantise_w1(b):
+            grouped = keep.tile([P, P, PACK], BF16, name="w1_grouped%d" % b, align_bytes=64)
+            planes = w1_raw[b // 2][:, :, (b % 2) * P : (b % 2 + 1) * P]
+            nc.scalar.activation(walk_words(grouped[:]), walk_planes(planes), ACT.Copy)
+            w1_q.append(quantise("w1_%d" % b, grouped))
+
+        quantise_w1(0)
+        quantise_w1(1)
+        tab_picked = gather("tab_picked", tab_window, U32)
+        quantise_w1(2)
+        quantise_w1(3)
+        query_grouped = keep.tile([P, P, PACK], BF16, name="query_grouped", align_bytes=64)
+        nc.vector.tensor_copy(walk_words(query_grouped[:]), walk_planes(query_raw[:]))
+        query_q = quantise("query", query_grouped)
+        keys_scale_picked = gather("keys_scale_picked", keys_scale_window, U8)
+
+        exps = []
+
+        def layer(b):
+            zh = psum.tile([P, SLOTS], F32, name="zh%d" % b, tag="bank%d" % b)
+            product(zh[:], w1_q[b], (tab_picked, tab_scale_picked))
+            ht = keep.tile([P, 2, P, 2], F32, name="ht%d" % b, tag=("w1_raw1", "ht1", "ht2", "ht3")[b])
+            nc.scalar.activation(
+                ht[:], zh[:].rearrange("r (p u h) -> r u p h", u=2, h=2), ACT.Exp, scale=temper_sb[:, b : b + 1]
+            )
+            exps.append(ht)
+
+        values_q = []
+        scaled_tiles = []
+        scaled_tags = ["scaled0", "scaled1", "grown", "scaled3"]
+
+        def invert(b, sums):
+            nc.vector.tensor_reduce(sums, exps[b][:].rearrange("r u (g e) h -> r g u (e h)", e=2), AXIS.XY, ALU.add)
+            nc.vector.reciprocal(spaced[b][:, 2 : 2 + 2 * GROUPS : 2], sums)
+
+        def turn(b):
+            ht = exps[b]
+            turned = psum.tile([P, PACK, P], F32, name="turned%d" % b, tag="bank%d" % (2, 3, 1, 1)[b])
+            for t in range(PACK):
+                nc.tensor.transpose(turned[:, t, :], ht[:, t // 2, :, t % 2], identity[:])
+            scaled = keep.tile([P, PACK, P], F32, name="scaled%d" % b, tag=scaled_tags[b])
+            for t in range(PACK):
+                nc.scalar.activation(scaled[:, t, :], turned[:, t, :], ACT.Copy, scale=vs4[:, t : t + 1])
+            scaled_tiles.append(scaled)
+
+        def normalise(b):
+            scaled = scaled_tiles[b]
+            inverse = psum.tile([P, P], F32, name="inverse%d" % b, tag="bank%d" % (4 + b % 2))
+            nc.tensor.matmul(inverse[:], spaced[b][:, 2 : 2 + P], identity[:], start=True, stop=False, is_transpose=True)
+            nc.tensor.matmul(inverse[:], spaced[b][:, 1 : 1 + P], identity[:], start=False, stop=True, is_transpose=True)
+            grouped = keep.tile([P, P, PACK], BF16, name="values_grouped%d" % b, tag="grouped%d" % b, align_bytes=64)
+            nc.vector.tensor_tensor(
+                walk_words(grouped[:]),
+                walk_planes(scaled[:]),
+                inverse[:].rearrange("p (c i) -> p c i", i=4).unsqueeze(2).to_broadcast([P, P // 4, PACK, 4]),
+                ALU.mult,
+            )
+            values_q.append(quantise("values%d" % b, grouped))
+
+        for b in range(BLOCKS):
+            layer(b)
+        first_sums = keep.tile([P, GROUPS], F32, name="first_sums")
+        invert(0, first_sums[:])
+        turn(0)
+        turn(1)
+
+        keys_picked = gather("keys_picked", keys_window, U32)
+        scores = psum.tile([P, SLOTS], F32, name="scores", tag="bank2")
+        product(scores[:], query_q, (keys_picked, keys_scale_picked))
+        grown = keep.tile([P, PACK, P], F32, name="grown", tag="grown")
+        nc.scalar.activation(grown[:], scores[:].rearrange("q (p t) -> q t p", t=PACK), ACT.Exp, bias=minus_th[:])
+        soft = keep.tile([P, PACK, P], F32, name="soft")
+        row_sum = keep.tile([P, 1], F32, name="row_sum")
+        nc.scalar.activation(soft[:], grown[:], ACT.Ln, bias=1.0, accum_out=row_sum[:])
+        turn(2)
+        total = keep.tile([P, 1], F32, name="total")
+        nc.vector.tensor_tensor(total[:], row_sum[:], reserve_sb[:], ALU.add)
+        share = keep.tile([P, 1], F32, name="share")
+        nc.vector.reciprocal(share[:], total[:])
+        weights = keep.tile([P, PACK, P], F32, name="weights")
+        nc.scalar.activation(weights[:], soft[:], ACT.Copy, scale=share[:])
+
+        turn(3)
+        later_sums = keep.tile([P, BLOCKS - 1, GROUPS], F32, name="later_sums", tag="keys_window", align_bytes=64)
+        invert(1, later_sums[:, 0, :])
+        normalise(0)
+        invert(2, later_sums[:, 1, :])
+        normalise(1)
+        invert(3, later_sums[:, 2, :])
+        normalise(2)
+
+        weights_turned = psum.tile([P, PACK, P], F32, name="weights_turned", tag="bank0")
+        for t in range(PACK):
+            nc.tensor.transpose(weights_turned[:, t, :], weights[:, t, :], identity[:])
+        weights_grouped = keep.tile([P, P, PACK], BF16, name="weights_grouped", align_bytes=64)
+        nc.vector.tensor_tensor(
+            weights_grouped[:],
+            weights_turned[:].rearrange("p t q -> p q t"),
+            os_sb[:].unsqueeze(1).to_broadcast([P, P, PACK]),
+            ALU.mult,
+        )
+        weights_q = quantise("weights", weights_grouped)
+
+        normalise(3)
+
+        for b in range(BLOCKS):
+            acc = psum.tile([P, P], F32, name="acc%d" % b, tag="bank%d" % (6, 7, 2, 3)[b])
+            product(acc[:], weights_q, values_q[b])
+            result = keep.tile([P, P], F32, name="result%d" % b)
+            nc.scalar.copy(result[:], acc[:])
+            nc.sync.dma_start(out[:, b * P : (b + 1) * P], result[:])

@@ -21,6 +21,7 @@ SLOTS = 512
 HIDDEN = 512
 GROUPS = 64
 BLOCKS = HIDDEN // P
+HALF = 2 * P
 FLOPS = 2 * 512 * 128 * 512 + 2 * 512 * 512 * 512 + 2 * 512 * 128 * 512
 
 
@@ -58,15 +59,16 @@ def tile_attend_lrshared_capped_kernel(
             nc.sync.dma_start(window[:].bitcast(I32), words[0].rearrange("p n t -> p (n t)").bitcast(I32))
             return window
 
-        def gather(name, window, dtype):
-            picked = keep.tile([P, SLOTS], dtype, name=name, align_bytes=64)
+        def gather(name, window, dtype, tag):
+            picked = keep.tile([P, SLOTS], dtype, name=name, tag=tag, align_bytes=64)
             nc.vector.tensor_copy(picked[:], window[:].indirect(offsets[:]))
             return picked
 
         def quantise(name, grouped):
-            codes = keep.tile([P, P], U32, name=name + "_codes", align_bytes=64)
-            scales = keep.tile([P, P], U8, name=name + "_scales", align_bytes=64)
-            nc.vector.quantize_mx(out=codes[:].bitcast(FP8X4), scales=scales[:], in_=grouped[:].rearrange("p c t -> p (c t)"))
+            width = grouped.shape[1]
+            codes = keep.tile([P, width], U32, name=name + "_codes", align_bytes=64)
+            scales = keep.tile([P, width], U8, name=name + "_scales", align_bytes=64)
+            nc.vector.quantize_mx(out=codes[:].bitcast(FP8X4), scales=scales[:], in_=grouped.rearrange("p c t -> p (c t)"))
             return codes, scales
 
         def product(acc, stationary, moving):
@@ -81,17 +83,17 @@ def tile_attend_lrshared_capped_kernel(
             )
 
         w1_rows = w1.rearrange("(p j) r -> p j r", j=PACK)
-        w1_raw = [keep.tile([P, PACK, 2 * P], F32, name="w1_raw%d" % half, tag="w1_raw%d" % half) for half in range(2)]
-        temper_sb = keep.tile([P, BLOCKS], F32, name="temper_sb")
+        w1_raw = [keep.tile([P, PACK, HALF], F32, name="w1_raw%d" % half, tag="w1_raw%d" % half) for half in range(2)]
+        temper_sb = keep.tile([P, BLOCKS], F32, name="temper_sb", tag="temper_sb", align_bytes=64)
         with nc.allow_non_contiguous_dma(reason="one temper value a partition and block"):
             nc.scalar.dma_start(temper_sb[:], temper.rearrange("(b p) o -> p (b o)", p=P))
-        nc.sync.dma_start(w1_raw[0][:], w1_rows[:, :, 0 : 2 * P])
+        nc.sync.dma_start(w1_raw[0][:], w1_rows[:, :, 0:HALF])
         tab_scale_window = load_scales(nc.sync, "tab_scale_window", tab_scales)
         tab_window = load_words("tab_window", tab_words)
-        nc.sync.dma_start(w1_raw[1][:], w1_rows[:, :, 2 * P : 4 * P])
-        query_raw = keep.tile([P, PACK, P], F32, name="query_raw", tag="query_raw")
-        nc.sync.dma_start(query_raw[:], query.rearrange("(p j) q -> p j q", j=PACK))
         keys_scale_window = load_scales(nc.sync, "keys_scale_window", keys_scales)
+        nc.sync.dma_start(w1_raw[1][:], w1_rows[:, :, HALF : 2 * HALF])
+        query_raw = keep.tile([P, PACK, P], F32, name="query_raw")
+        nc.sync.dma_start(query_raw[:], query.rearrange("(p j) q -> p j q", j=PACK))
         keys_window = load_words("keys_window", keys_words)
         vs_sb = keep.tile([P, PACK], F32, name="vs_sb")
         nc.sync.dma_start(vs_sb[:], value_scale.rearrange("o (p t) -> (o p) t", t=PACK))
@@ -104,15 +106,17 @@ def tile_attend_lrshared_capped_kernel(
 
         identity = keep.tile([P, P], F32, name="identity")
         make_identity(nc, identity[:])
-        spaced = [keep.tile([P, 2 * GROUPS + 8], F32, name="spaced%d" % b) for b in range(BLOCKS)]
-        for b in range(BLOCKS):
-            nc.gpsimd.memset(spaced[b][:], 0.0)
+        spaced = [keep.tile([P, 2, 2 * GROUPS + 8], F32, name="spaced%d" % half) for half in range(2)]
+        for half in range(2):
+            nc.gpsimd.memset(spaced[half][:], 0.0)
+        minus_one = keep.tile([P, 1], F32, name="minus_one")
+        nc.gpsimd.memset(minus_one[:], -1.0)
         vs4 = keep.tile([P, PACK], F32, name="vs4")
         nc.gpsimd.tensor_scalar(vs4[:], vs_sb[:], 4.0, 0.0, ALU.mult, ALU.add)
         minus_th = keep.tile([P, 1], F32, name="minus_th")
         nc.gpsimd.tensor_scalar(minus_th[:], th_sb[:], -1.0, 0.0, ALU.mult, ALU.add)
 
-        tab_scale_picked = gather("tab_scale_picked", tab_scale_window, U8)
+        tab_scale_picked = gather("tab_scale_picked", tab_scale_window, U8, "tab_scale_picked")
 
         w1_q = []
 
@@ -120,94 +124,86 @@ def tile_attend_lrshared_capped_kernel(
             grouped = keep.tile([P, P, PACK], BF16, name="w1_grouped%d" % b, align_bytes=64)
             planes = w1_raw[b // 2][:, :, (b % 2) * P : (b % 2 + 1) * P]
             nc.scalar.activation(walk_words(grouped[:]), walk_planes(planes), ACT.Copy)
-            w1_q.append(quantise("w1_%d" % b, grouped))
+            w1_q.append(quantise("w1_%d" % b, grouped[:]))
 
         quantise_w1(0)
         quantise_w1(1)
-        tab_picked = gather("tab_picked", tab_window, U32)
+        tab_picked = gather("tab_picked", tab_window, U32, "tab_picked")
         quantise_w1(2)
         quantise_w1(3)
+        keys_scale_picked = gather("keys_scale_picked", keys_scale_window, U8, "keys_scale_picked")
         query_grouped = keep.tile([P, P, PACK], BF16, name="query_grouped", align_bytes=64)
         nc.vector.tensor_copy(walk_words(query_grouped[:]), walk_planes(query_raw[:]))
-        query_q = quantise("query", query_grouped)
-        keys_scale_picked = gather("keys_scale_picked", keys_scale_window, U8)
+        query_q = quantise("query", query_grouped[:])
 
-        exps = []
-
-        def layer(b):
+        exps = [keep.tile([P, 2, 2, P, 2], F32, name="ht%d" % half, tag=("w1_raw1", "ht1")[half]) for half in range(2)]
+        for b in range(BLOCKS):
             zh = psum.tile([P, SLOTS], F32, name="zh%d" % b, tag="bank%d" % b)
             product(zh[:], w1_q[b], (tab_picked, tab_scale_picked))
-            ht = keep.tile([P, 2, P, 2], F32, name="ht%d" % b, tag=("w1_raw1", "ht1", "ht2", "ht3")[b])
             nc.scalar.activation(
-                ht[:], zh[:].rearrange("r (p u h) -> r u p h", u=2, h=2), ACT.Exp, scale=temper_sb[:, b : b + 1]
+                exps[b // 2][:, :, b % 2, :, :],
+                zh[:].rearrange("r (p u h) -> r u p h", u=2, h=2),
+                ACT.Exp,
+                scale=temper_sb[:, b : b + 1],
             )
-            exps.append(ht)
 
-        values_q = []
-        scaled_tiles = []
-        scaled_tags = ["scaled0", "scaled1", "grown", "scaled3"]
+        def group_sums(half):
+            sums = keep.tile([P, 2 * GROUPS], F32, name="sums%d" % half)
+            nc.vector.tensor_reduce(sums[:], exps[half][:].rearrange("r u b (g e) h -> r (b g) u (e h)", e=2), AXIS.XY, ALU.add)
+            return sums
 
-        def invert(b, sums):
-            nc.vector.tensor_reduce(sums, exps[b][:].rearrange("r u (g e) h -> r g u (e h)", e=2), AXIS.XY, ALU.add)
-            nc.vector.reciprocal(spaced[b][:, 2 : 2 + 2 * GROUPS : 2], sums)
+        def invert(half, sums):
+            nc.vector.reciprocal(spaced[half][:, :, 2 : 2 + 2 * GROUPS : 2], sums[:].rearrange("r (b g) -> r b g", b=2))
+            inverse = psum.tile([P, HALF], F32, name="inverse%d" % half, tag="bank%d" % (5 + half))
+            for b in range(2):
+                columns = inverse[:, b * P : (b + 1) * P]
+                nc.tensor.matmul(columns, spaced[half][:, b, 2 : 2 + P], identity[:], start=True, stop=False, is_transpose=True)
+                nc.tensor.matmul(columns, spaced[half][:, b, 1 : 1 + P], identity[:], start=False, stop=True, is_transpose=True)
+            return inverse
 
-        def turn(b):
-            ht = exps[b]
-            turned = psum.tile([P, PACK, P], F32, name="turned%d" % b, tag="bank%d" % (2, 3, 1, 1)[b])
+        def turn(half, banks):
+            turned = [psum.tile([P, 2, HALF], F32, name="turned%d_%d" % (half, u), tag=banks[u]) for u in range(2)]
+            for u in range(2):
+                for h in range(2):
+                    for b in range(2):
+                        nc.tensor.transpose(turned[u][:, h, b * P : (b + 1) * P], exps[half][:, u, b, :, h], identity[:])
+            return turned
+
+        def scale_values(half, turned, tag):
+            scaled = keep.tile([P, PACK, HALF], F32, name="scaled%d" % half, tag=tag)
             for t in range(PACK):
-                nc.tensor.transpose(turned[:, t, :], ht[:, t // 2, :, t % 2], identity[:])
-            scaled = keep.tile([P, PACK, P], F32, name="scaled%d" % b, tag=scaled_tags[b])
-            for t in range(PACK):
-                nc.scalar.activation(scaled[:, t, :], turned[:, t, :], ACT.Copy, scale=vs4[:, t : t + 1])
-            scaled_tiles.append(scaled)
+                nc.scalar.activation(scaled[:, t, :], turned[t // 2][:, t % 2, :], ACT.Copy, scale=vs4[:, t : t + 1])
+            return scaled
 
-        def normalise(b):
-            scaled = scaled_tiles[b]
-            inverse = psum.tile([P, P], F32, name="inverse%d" % b, tag="bank%d" % (4 + b % 2))
-            nc.tensor.matmul(inverse[:], spaced[b][:, 2 : 2 + P], identity[:], start=True, stop=False, is_transpose=True)
-            nc.tensor.matmul(inverse[:], spaced[b][:, 1 : 1 + P], identity[:], start=False, stop=True, is_transpose=True)
-            grouped = keep.tile([P, P, PACK], BF16, name="values_grouped%d" % b, tag="grouped%d" % b, align_bytes=64)
+        def normalise(name, scaled, inverse):
+            width = inverse.shape[1]
+            grouped = keep.tile([P, width, PACK], BF16, name=name + "_grouped", align_bytes=64)
             nc.vector.tensor_tensor(
                 walk_words(grouped[:]),
-                walk_planes(scaled[:]),
-                inverse[:].rearrange("p (c i) -> p c i", i=4).unsqueeze(2).to_broadcast([P, P // 4, PACK, 4]),
+                walk_planes(scaled),
+                inverse.rearrange("p (c i) -> p c i", i=4).unsqueeze(2).to_broadcast([P, width // 4, PACK, 4]),
                 ALU.mult,
             )
-            values_q.append(quantise("values%d" % b, grouped))
+            return quantise(name, grouped[:])
 
-        for b in range(BLOCKS):
-            layer(b)
-        first_sums = keep.tile([P, GROUPS], F32, name="first_sums")
-        invert(0, first_sums[:])
-        turn(0)
-        turn(1)
+        sums0 = group_sums(0)
+        scaled0 = scale_values(0, turn(0, ("bank1", "bank0")), "scaled0")
 
-        keys_picked = gather("keys_picked", keys_window, U32)
-        scores = psum.tile([P, SLOTS], F32, name="scores", tag="bank2")
+        keys_picked = gather("keys_picked", keys_window, U32, "temper_sb")
+        scores = psum.tile([P, SLOTS], F32, name="scores", tag="bank4")
         product(scores[:], query_q, (keys_picked, keys_scale_picked))
         grown = keep.tile([P, PACK, P], F32, name="grown", tag="grown")
         nc.scalar.activation(grown[:], scores[:].rearrange("q (p t) -> q t p", t=PACK), ACT.Exp, bias=minus_th[:])
         soft = keep.tile([P, PACK, P], F32, name="soft")
         row_sum = keep.tile([P, 1], F32, name="row_sum")
         nc.scalar.activation(soft[:], grown[:], ACT.Ln, bias=1.0, accum_out=row_sum[:])
-        turn(2)
         total = keep.tile([P, 1], F32, name="total")
-        nc.vector.tensor_tensor(total[:], row_sum[:], reserve_sb[:], ALU.add)
+        nc.gpsimd.tensor_tensor(total[:], row_sum[:], reserve_sb[:], ALU.add)
         share = keep.tile([P, 1], F32, name="share")
-        nc.vector.reciprocal(share[:], total[:])
+        nc.gpsimd.tensor_tensor(share[:], total[:], minus_one[:], ALU.pow)
         weights = keep.tile([P, PACK, P], F32, name="weights")
         nc.scalar.activation(weights[:], soft[:], ACT.Copy, scale=share[:])
-
-        turn(3)
-        later_sums = keep.tile([P, BLOCKS - 1, GROUPS], F32, name="later_sums", tag="keys_window", align_bytes=64)
-        invert(1, later_sums[:, 0, :])
-        normalise(0)
-        invert(2, later_sums[:, 1, :])
-        normalise(1)
-        invert(3, later_sums[:, 2, :])
-        normalise(2)
-
-        weights_turned = psum.tile([P, PACK, P], F32, name="weights_turned", tag="bank0")
+        weights_turned = psum.tile([P, PACK, P], F32, name="weights_turned", tag="bank7")
         for t in range(PACK):
             nc.tensor.transpose(weights_turned[:, t, :], weights[:, t, :], identity[:])
         weights_grouped = keep.tile([P, P, PACK], BF16, name="weights_grouped", align_bytes=64)
@@ -217,13 +213,25 @@ def tile_attend_lrshared_capped_kernel(
             os_sb[:].unsqueeze(1).to_broadcast([P, P, PACK]),
             ALU.mult,
         )
-        weights_q = quantise("weights", weights_grouped)
+        weights_q = quantise("weights", weights_grouped[:])
 
-        normalise(3)
+        turned1 = turn(1, ("bank2", "bank3"))
+        inverse0 = invert(0, sums0)
+        inverse1 = invert(1, group_sums(1))
+        scaled1 = scale_values(1, turned1, "grown")
 
-        for b in range(BLOCKS):
-            acc = psum.tile([P, P], F32, name="acc%d" % b, tag="bank%d" % (6, 7, 2, 3)[b])
-            product(acc[:], weights_q, values_q[b])
-            result = keep.tile([P, P], F32, name="result%d" % b)
-            nc.scalar.copy(result[:], acc[:])
-            nc.sync.dma_start(out[:, b * P : (b + 1) * P], result[:])
+        pieces = [
+            (0, HALF, scaled0[:], inverse0[:], "bank4"),
+            (HALF, P, scaled1[:, :, 0:P], inverse1[:, 0:P], "bank0"),
+            (HALF + P, P, scaled1[:, :, P:HALF], inverse1[:, P:HALF], "bank1"),
+        ]
+        for first, width, scaled, inverse, bank in pieces:
+            values_q = normalise("values%d" % first, scaled, inverse)
+            acc = psum.tile([P, width], F32, name="acc%d" % first, tag=bank)
+            product(acc[:], weights_q, values_q)
+            result = keep.tile([P, width], F32, name="result%d" % first)
+            if first == HALF + P:
+                nc.vector.tensor_copy(result[:], acc[:])
+            else:
+                nc.scalar.copy(result[:], acc[:])
+            nc.sync.dma_start(out[:, first : first + width], result[:])

@@ -22,15 +22,18 @@ HIDDEN = 512
 GROUPS = 64
 BLOCKS = HIDDEN // P
 HALF = 2 * P
+RUN = 4
+LEAD = 2
+SPACED = 2 * GROUPS + 8
 FLOPS = 2 * 512 * 128 * 512 + 2 * 512 * 512 * 512 + 2 * 512 * 128 * 512
 
 
 def walk_planes(ap):
-    return ap.rearrange("p t (c i) -> p c t i", i=4)
+    return ap.rearrange("p t (c i) -> p c t i", i=RUN)
 
 
 def walk_words(ap):
-    return ap.rearrange("p (c i) t -> p c t i", i=4)
+    return ap.rearrange("p (c i) t -> p c t i", i=RUN)
 
 
 def tile_attend_lrshared_capped_kernel(
@@ -45,22 +48,22 @@ def tile_attend_lrshared_capped_kernel(
         offsets = lists.tile([P, SLOTS // 16], U16, name="offsets")
         nc.sync.dma_start(offsets[:], offs)
 
-        def load_scales(queue, name, scales):
+        def load_scales(name, scales):
             window = keep.tile([P, POOL], U8, name=name, align_bytes=64)
             nc.vector.memset(window[:].bitcast(I32), 0)
             for quad in range(4):
-                queue.dma_start(
+                nc.sync.dma_start(
                     window[32 * quad : 32 * quad + 4, :].bitcast(I32), scales[0, 4 * quad : 4 * quad + 4, :].bitcast(I32)
                 )
             return window
 
         def load_words(name, words):
-            window = keep.tile([P, POOL], U32, name=name, tag=name, align_bytes=64)
+            window = keep.tile([P, POOL], U32, name=name, align_bytes=64)
             nc.sync.dma_start(window[:].bitcast(I32), words[0].rearrange("p n t -> p (n t)").bitcast(I32))
             return window
 
-        def gather(name, window, dtype, tag):
-            picked = keep.tile([P, SLOTS], dtype, name=name, tag=tag, align_bytes=64)
+        def gather(name, window, dtype):
+            picked = keep.tile([P, SLOTS], dtype, name=name, align_bytes=64)
             nc.vector.tensor_copy(picked[:], window[:].indirect(offsets[:]))
             return picked
 
@@ -84,39 +87,44 @@ def tile_attend_lrshared_capped_kernel(
 
         w1_rows = w1.rearrange("(p j) r -> p j r", j=PACK)
         w1_raw = [keep.tile([P, PACK, HALF], F32, name="w1_raw%d" % half, tag="w1_raw%d" % half) for half in range(2)]
-        temper_sb = keep.tile([P, BLOCKS], F32, name="temper_sb", tag="temper_sb", align_bytes=64)
-        with nc.allow_non_contiguous_dma(reason="one temper value a partition and block"):
-            nc.scalar.dma_start(temper_sb[:], temper.rearrange("(b p) o -> p (b o)", p=P))
+        temper_sb = keep.tile([P, BLOCKS], F32, name="temper_sb", align_bytes=64)
+        temper_rows = keep.tile([P, P], F32, name="temper_rows")
+        nc.gpsimd.memset(temper_rows[:], 0.0)
+        nc.gpsimd.dma_start(temper_rows[0:BLOCKS, :], temper.rearrange("(b p) o -> b (p o)", p=P))
         nc.sync.dma_start(w1_raw[0][:], w1_rows[:, :, 0:HALF])
-        tab_scale_window = load_scales(nc.sync, "tab_scale_window", tab_scales)
+        tab_scale_window = load_scales("tab_scale_window", tab_scales)
         tab_window = load_words("tab_window", tab_words)
-        keys_scale_window = load_scales(nc.sync, "keys_scale_window", keys_scales)
+        keys_scale_window = load_scales("keys_scale_window", keys_scales)
         nc.sync.dma_start(w1_raw[1][:], w1_rows[:, :, HALF : 2 * HALF])
         query_raw = keep.tile([P, PACK, P], F32, name="query_raw")
         nc.sync.dma_start(query_raw[:], query.rearrange("(p j) q -> p j q", j=PACK))
         keys_window = load_words("keys_window", keys_words)
-        vs_sb = keep.tile([P, PACK], F32, name="vs_sb")
-        nc.sync.dma_start(vs_sb[:], value_scale.rearrange("o (p t) -> (o p) t", t=PACK))
-        th_sb = keep.tile([P, 1], F32, name="th_sb")
-        nc.sync.dma_start(th_sb[:], th)
-        os_sb = keep.tile([P, PACK], F32, name="os_sb")
-        nc.sync.dma_start(os_sb[:], slot_factor.rearrange("o (p t) -> (o p) t", t=PACK))
-        reserve_sb = keep.tile([P, 1], F32, name="reserve_sb")
-        nc.sync.dma_start(reserve_sb[:], reserve)
 
         identity = keep.tile([P, P], F32, name="identity")
         make_identity(nc, identity[:])
-        spaced = [keep.tile([P, 2, 2 * GROUPS + 8], F32, name="spaced%d" % half) for half in range(2)]
+        temper_turned = psum.tile([P, P], F32, name="temper_turned", tag="bank7")
+        nc.tensor.transpose(temper_turned[:], temper_rows[:], identity[:])
+        nc.scalar.copy(temper_sb[:], temper_turned[:, 0:BLOCKS])
+        spaced = [keep.tile([P, 2, SPACED], F32, name="spaced%d" % half) for half in range(2)]
         for half in range(2):
             nc.gpsimd.memset(spaced[half][:], 0.0)
         minus_one = keep.tile([P, 1], F32, name="minus_one")
         nc.gpsimd.memset(minus_one[:], -1.0)
+        vs_sb = keep.tile([P, PACK], F32, name="vs_sb")
+        nc.gpsimd.dma_start(vs_sb[:], value_scale.rearrange("o (p t) -> (o p) t", t=PACK))
+        th_sb = keep.tile([P, 1], F32, name="th_sb")
+        nc.gpsimd.dma_start(th_sb[:], th)
+        os_sb = keep.tile([P, PACK], F32, name="os_sb")
+        nc.gpsimd.dma_start(os_sb[:], slot_factor.rearrange("o (p t) -> (o p) t", t=PACK))
+        reserve_sb = keep.tile([P, 1], F32, name="reserve_sb")
+        nc.gpsimd.dma_start(reserve_sb[:], reserve)
+
         vs4 = keep.tile([P, PACK], F32, name="vs4")
         nc.gpsimd.tensor_scalar(vs4[:], vs_sb[:], 4.0, 0.0, ALU.mult, ALU.add)
         minus_th = keep.tile([P, 1], F32, name="minus_th")
         nc.gpsimd.tensor_scalar(minus_th[:], th_sb[:], -1.0, 0.0, ALU.mult, ALU.add)
 
-        tab_scale_picked = gather("tab_scale_picked", tab_scale_window, U8, "tab_scale_picked")
+        tab_scale_picked = gather("tab_scale_picked", tab_scale_window, U8)
 
         w1_q = []
 
@@ -128,10 +136,10 @@ def tile_attend_lrshared_capped_kernel(
 
         quantise_w1(0)
         quantise_w1(1)
-        tab_picked = gather("tab_picked", tab_window, U32, "tab_picked")
+        tab_picked = gather("tab_picked", tab_window, U32)
         quantise_w1(2)
         quantise_w1(3)
-        keys_scale_picked = gather("keys_scale_picked", keys_scale_window, U8, "keys_scale_picked")
+        keys_scale_picked = gather("keys_scale_picked", keys_scale_window, U8)
         query_grouped = keep.tile([P, P, PACK], BF16, name="query_grouped", align_bytes=64)
         nc.vector.tensor_copy(walk_words(query_grouped[:]), walk_planes(query_raw[:]))
         query_q = quantise("query", query_grouped[:])
@@ -149,16 +157,20 @@ def tile_attend_lrshared_capped_kernel(
 
         def group_sums(half):
             sums = keep.tile([P, 2 * GROUPS], F32, name="sums%d" % half)
-            nc.vector.tensor_reduce(sums[:], exps[half][:].rearrange("r u b (g e) h -> r (b g) u (e h)", e=2), AXIS.XY, ALU.add)
+            pairs = keep.tile([P, 2 * GROUPS, PACK], F32, name="pairs%d" % half)
+            planes = exps[half][:].rearrange("r u b p h -> r u (b p h)")
+            nc.gpsimd.tensor_tensor(pairs[:].rearrange("r c x -> r (c x)"), planes[:, 0, :], planes[:, 1, :], ALU.add)
+            nc.vector.tensor_reduce(sums[:], pairs[:], AXIS.X, ALU.add)
             return sums
 
         def invert(half, sums):
-            nc.vector.reciprocal(spaced[half][:, :, 2 : 2 + 2 * GROUPS : 2], sums[:].rearrange("r (b g) -> r b g", b=2))
+            nc.vector.reciprocal(spaced[half][:, :, LEAD : LEAD + 2 * GROUPS : 2], sums[:].rearrange("r (b g) -> r b g", b=2))
             inverse = psum.tile([P, HALF], F32, name="inverse%d" % half, tag="bank%d" % (5 + half))
             for b in range(2):
                 columns = inverse[:, b * P : (b + 1) * P]
-                nc.tensor.matmul(columns, spaced[half][:, b, 2 : 2 + P], identity[:], start=True, stop=False, is_transpose=True)
-                nc.tensor.matmul(columns, spaced[half][:, b, 1 : 1 + P], identity[:], start=False, stop=True, is_transpose=True)
+                for shift in range(2):
+                    row = spaced[half][:, b, LEAD - shift : LEAD - shift + P]
+                    nc.tensor.matmul(columns, row, identity[:], start=(shift == 0), stop=(shift == 1), is_transpose=True)
             return inverse
 
         def turn(half, banks):
@@ -181,7 +193,7 @@ def tile_attend_lrshared_capped_kernel(
             nc.vector.tensor_tensor(
                 walk_words(grouped[:]),
                 walk_planes(scaled),
-                inverse.rearrange("p (c i) -> p c i", i=4).unsqueeze(2).to_broadcast([P, width // 4, PACK, 4]),
+                inverse.rearrange("p (c i) -> p c i", i=RUN).unsqueeze(2).to_broadcast([P, width // RUN, PACK, RUN]),
                 ALU.mult,
             )
             return quantise(name, grouped[:])
@@ -189,7 +201,7 @@ def tile_attend_lrshared_capped_kernel(
         sums0 = group_sums(0)
         scaled0 = scale_values(0, turn(0, ("bank1", "bank0")), "scaled0")
 
-        keys_picked = gather("keys_picked", keys_window, U32, "temper_sb")
+        keys_picked = gather("keys_picked", keys_window, U32)
         scores = psum.tile([P, SLOTS], F32, name="scores", tag="bank4")
         product(scores[:], query_q, (keys_picked, keys_scale_picked))
         grown = keep.tile([P, PACK, P], F32, name="grown", tag="grown")
@@ -198,7 +210,7 @@ def tile_attend_lrshared_capped_kernel(
         row_sum = keep.tile([P, 1], F32, name="row_sum")
         nc.scalar.activation(soft[:], grown[:], ACT.Ln, bias=1.0, accum_out=row_sum[:])
         total = keep.tile([P, 1], F32, name="total")
-        nc.gpsimd.tensor_tensor(total[:], row_sum[:], reserve_sb[:], ALU.add)
+        nc.scalar.activation(total[:], row_sum[:], ACT.Identity, bias=reserve_sb[:])
         share = keep.tile([P, 1], F32, name="share")
         nc.gpsimd.tensor_tensor(share[:], total[:], minus_one[:], ALU.pow)
         weights = keep.tile([P, PACK, P], F32, name="weights")
@@ -220,18 +232,11 @@ def tile_attend_lrshared_capped_kernel(
         inverse1 = invert(1, group_sums(1))
         scaled1 = scale_values(1, turned1, "grown")
 
-        pieces = [
-            (0, HALF, scaled0[:], inverse0[:], "bank4"),
-            (HALF, P, scaled1[:, :, 0:P], inverse1[:, 0:P], "bank0"),
-            (HALF + P, P, scaled1[:, :, P:HALF], inverse1[:, P:HALF], "bank1"),
-        ]
-        for first, width, scaled, inverse, bank in pieces:
-            values_q = normalise("values%d" % first, scaled, inverse)
-            acc = psum.tile([P, width], F32, name="acc%d" % first, tag=bank)
+        halves = [(scaled0, inverse0, "bank4", nc.scalar.copy), (scaled1, inverse1, "bank0", nc.vector.tensor_copy)]
+        for half, (scaled, inverse, bank, copy_out) in enumerate(halves):
+            values_q = normalise("values%d" % half, scaled[:], inverse[:])
+            acc = psum.tile([P, HALF], F32, name="acc%d" % half, tag=bank)
             product(acc[:], weights_q, values_q)
-            result = keep.tile([P, width], F32, name="result%d" % first)
-            if first == HALF + P:
-                nc.vector.tensor_copy(result[:], acc[:])
-            else:
-                nc.scalar.copy(result[:], acc[:])
-            nc.sync.dma_start(out[:, first : first + width], result[:])
+            result = keep.tile([P, HALF], F32, name="result%d" % half)
+            copy_out(result[:], acc[:])
+            nc.sync.dma_start(out[:, half * HALF : (half + 1) * HALF], result[:])

from contextlib import ExitStack

import concourse.mybir as mybir
from concourse.masks import make_identity

F32 = mybir.dt.float32
BF16 = mybir.dt.bfloat16
I32 = mybir.dt.int32
U32 = mybir.dt.uint32
U16 = mybir.dt.uint16
U8 = mybir.dt.uint8
FP8X4 = mybir.dt.float8_e4m3fn_x4
ACT = mybir.ActivationFunctionType
ALU = mybir.AluOpType
AXIS = mybir.AxisListType

P = 128
PACK = 4
POOL = 2048
SLOTS = 512
HIDDEN = 512
GROUPS = 64
BLOCKS = HIDDEN // P
HALF = 2 * P
RUN = 4
LEAD = 2
SPACED = 2 * GROUPS + 8
FLOPS = 2 * 512 * 128 * 512 + 2 * 512 * 512 * 512 + 2 * 512 * 128 * 512


def walk_planes(ap):
    return ap.rearrange("p t (c i) -> p c t i", i=RUN)


def walk_words(ap):
    return ap.rearrange("p (c i) t -> p c t i", i=RUN)


def tile_attend_lrshared_capped_kernel(
    tc, query, keys_words, keys_scales, th, reserve, tab_words, tab_scales, w1, temper, slot_factor, value_scale, offs, out
):
    nc = tc.nc
    with ExitStack() as ctx:
        lists = ctx.enter_context(tc.tile_pool(name="lists", bufs=1))
        keep = ctx.enter_context(tc.tile_pool(name="keep", bufs=1))
        psum = ctx.enter_context(tc.psum_pool(name="psum", bufs=1))

        offsets = lists.tile([P, SLOTS // 16], U16, name="offsets")
        nc.sync.dma_start(offsets[:], offs)

        def load_scales(name, scales):
            window = keep.tile([P, POOL], U8, name=name, align_bytes=64)
            nc.vector.memset(window[:].bitcast(I32), 0)
            for quad in range(4):
                nc.sync.dma_start(
                    window[32 * quad : 32 * quad + 4, :].bitcast(I32), scales[0, 4 * quad : 4 * quad + 4, :].bitcast(I32)
                )
            return window

        def load_words(name, words):
            window = keep.tile([P, POOL], U32, name=name, align_bytes=64)
            nc.sync.dma_start(window[:].bitcast(I32), words[0].rearrange("p n t -> p (n t)").bitcast(I32))
            return window

        def gather(name, window, dtype):
            picked = keep.tile([P, SLOTS], dtype, name=name, align_bytes=64)
            nc.vector.tensor_copy(picked[:], window[:].indirect(offsets[:]))
            return picked

        def quantise(name, grouped):
            width = grouped.shape[1]
            codes = keep.tile([P, width], U32, name=name + "_codes", align_bytes=64)
            scales = keep.tile([P, width], U8, name=name + "_scales", align_bytes=64)
            nc.vector.quantize_mx(out=codes[:].bitcast(FP8X4), scales=scales[:], in_=grouped.rearrange("p c t -> p (c t)"))
            return codes, scales

        def product(acc, stationary, moving):
            nc.tensor.matmul_mx(
                out=acc,
                lhsT=stationary[0][:].bitcast(FP8X4),
                lhsT_scale=stationary[1][:],
                rhs=moving[0][:].bitcast(FP8X4),
                rhs_scale=moving[1][:],
                start=True,
                stop=True,
            )

        w1_rows = w1.rearrange("(p j) r -> p j r", j=PACK)
        w1_raw = [keep.tile([P, PACK, HALF], F32, name="w1_raw%d" % half, tag="w1_raw%d" % half) for half in range(2)]
        temper_sb = keep.tile([P, BLOCKS], F32, name="temper_sb", align_bytes=64)
        temper_rows = keep.tile([P, P], F32, name="temper_rows")
        nc.gpsimd.memset(temper_rows[:], 0.0)
        nc.gpsimd.dma_start(temper_rows[0:BLOCKS, :], temper.rearrange("(b p) o -> b (p o)", p=P))
        nc.sync.dma_start(w1_raw[0][:], w1_rows[:, :, 0:HALF])
        tab_scale_window = load_scales("tab_scale_window", tab_scales)
        tab_window = load_words("tab_window", tab_words)
        keys_scale_window = load_scales("keys_scale_window", keys_scales)
        nc.sync.dma_start(w1_raw[1][:], w1_rows[:, :, HALF : 2 * HALF])
        query_raw = keep.tile([P, PACK, P], F32, name="query_raw")
        nc.sync.dma_start(query_raw[:], query.rearrange("(p j) q -> p j q", j=PACK))
        keys_window = load_words("keys_window", keys_words)

        identity = keep.tile([P, P], F32, name="identity")
        make_identity(nc, identity[:])
        temper_turned = psum.tile([P, P], F32, name="temper_turned", tag="bank7")
        nc.tensor.transpose(temper_turned[:], temper_rows[:], identity[:])
        nc.scalar.copy(temper_sb[:], temper_turned[:, 0:BLOCKS])
        spaced = [keep.tile([P, 2, SPACED], F32, name="spaced%d" % half) for half in range(2)]
        for half in range(2):
            nc.gpsimd.memset(spaced[half][:], 0.0)
        minus_one = keep.tile([P, 1], F32, name="minus_one")
        nc.gpsimd.memset(minus_one[:], -1.0)
        vs_sb = keep.tile([P, PACK], F32, name="vs_sb")
        nc.gpsimd.dma_start(vs_sb[:], value_scale.rearrange("o (p t) -> (o p) t", t=PACK))
        th_sb = keep.tile([P, 1], F32, name="th_sb")
        nc.gpsimd.dma_start(th_sb[:], th)
        os_sb = keep.tile([P, PACK], F32, name="os_sb")
        nc.gpsimd.dma_start(os_sb[:], slot_factor.rearrange("o (p t) -> (o p) t", t=PACK))
        reserve_sb = keep.tile([P, 1], F32, name="reserve_sb")
        nc.gpsimd.dma_start(reserve_sb[:], reserve)

        vs4 = keep.tile([P, PACK], F32, name="vs4")
        nc.gpsimd.tensor_scalar(vs4[:], vs_sb[:], 4.0, 0.0, ALU.mult, ALU.add)
        minus_th = keep.tile([P, 1], F32, name="minus_th")
        nc.gpsimd.tensor_scalar(minus_th[:], th_sb[:], -1.0, 0.0, ALU.mult, ALU.add)

        tab_scale_picked = gather("tab_scale_picked", tab_scale_window, U8)

        w1_q = []

        def quantise_w1(b):
            grouped = keep.tile([P, P, PACK], BF16, name="w1_grouped%d" % b, align_bytes=64)
            planes = w1_raw[b // 2][:, :, (b % 2) * P : (b % 2 + 1) * P]
            nc.scalar.activation(walk_words(grouped[:]), walk_planes(planes), ACT.Copy)
            w1_q.append(quantise("w1_%d" % b, grouped[:]))

        quantise_w1(0)
        quantise_w1(1)
        tab_picked = gather("tab_picked", tab_window, U32)
        quantise_w1(2)
        quantise_w1(3)
        keys_scale_picked = gather("keys_scale_picked", keys_scale_window, U8)
        query_grouped = keep.tile([P, P, PACK], BF16, name="query_grouped", align_bytes=64)
        nc.vector.tensor_copy(walk_words(query_grouped[:]), walk_planes(query_raw[:]))
        query_q = quantise("query", query_grouped[:])

        exps = [keep.tile([P, 2, 2, P, 2], F32, name="ht%d" % half, tag=("w1_raw1", "ht1")[half]) for half in range(2)]
        for b in range(BLOCKS):
            zh = psum.tile([P, SLOTS], F32, name="zh%d" % b, tag="bank%d" % b)
            product(zh[:], w1_q[b], (tab_picked, tab_scale_picked))
            nc.scalar.activation(
                exps[b // 2][:, :, b % 2, :, :],
                zh[:].rearrange("r (p u h) -> r u p h", u=2, h=2),
                ACT.Exp,
                scale=temper_sb[:, b : b + 1],
            )

        def group_sums(half):
            sums = keep.tile([P, 2 * GROUPS], F32, name="sums%d" % half)
            pairs = keep.tile([P, 2 * GROUPS, PACK], F32, name="pairs%d" % half)
            planes = exps[half][:].rearrange("r u b p h -> r u (b p h)")
            nc.gpsimd.tensor_tensor(pairs[:].rearrange("r c x -> r (c x)"), planes[:, 0, :], planes[:, 1, :], ALU.add)
            nc.vector.tensor_reduce(sums[:], pairs[:], AXIS.X, ALU.add)
            return sums

        def invert(half, sums):
            nc.vector.reciprocal(spaced[half][:, :, LEAD : LEAD + 2 * GROUPS : 2], sums[:].rearrange("r (b g) -> r b g", b=2))
            inverse = psum.tile([P, HALF], F32, name="inverse%d" % half, tag="bank%d" % (5 + half))
            for b in range(2):
                columns = inverse[:, b * P : (b + 1) * P]
                for shift in range(2):
                    row = spaced[half][:, b, LEAD - shift : LEAD - shift + P]
                    nc.tensor.matmul(columns, row, identity[:], start=(shift == 0), stop=(shift == 1), is_transpose=True)
            return inverse

        def turn(half, banks):
            turned = [psum.tile([P, 2, HALF], F32, name="turned%d_%d" % (half, u), tag=banks[u]) for u in range(2)]
            for u in range(2):
                for h in range(2):
                    for b in range(2):
                        nc.tensor.transpose(turned[u][:, h, b * P : (b + 1) * P], exps[half][:, u, b, :, h], identity[:])
            return turned

        def scale_values(half, turned, tag):
            scaled = keep.tile([P, PACK, HALF], F32, name="scaled%d" % half, tag=tag)
            for t in range(PACK):
                nc.scalar.activation(scaled[:, t, :], turned[t // 2][:, t % 2, :], ACT.Copy, scale=vs4[:, t : t + 1])
            return scaled

        def normalise(name, scaled, inverse):
            width = inverse.shape[1]
            grouped = keep.tile([P, width, PACK], BF16, name=name + "_grouped", align_bytes=64)
            nc.vector.tensor_tensor(
                walk_words(grouped[:]),
                walk_planes(scaled),
                inverse.rearrange("p (c i) -> p c i", i=RUN).unsqueeze(2).to_broadcast([P, width // RUN, PACK, RUN]),
                ALU.mult,
            )
            return quantise(name, grouped[:])

        sums0 = group_sums(0)
        scaled0 = scale_values(0, turn(0, ("bank1", "bank0")), "scaled0")

        keys_picked = gather("keys_picked", keys_window, U32)
        scores = psum.tile([P, SLOTS], F32, name="scores", tag="bank4")
        product(scores[:], query_q, (keys_picked, keys_scale_picked))
        grown = keep.tile([P, PACK, P], F32, name="grown", tag="grown")
        nc.scalar.activation(grown[:], scores[:].rearrange("q (p t) -> q t p", t=PACK), ACT.Exp, bias=minus_th[:])
        soft = keep.tile([P, PACK, P], F32, name="soft")
        row_sum = keep.tile([P, 1], F32, name="row_sum")
        nc.scalar.activation(soft[:], grown[:], ACT.Ln, bias=1.0, accum_out=row_sum[:])
        total = keep.tile([P, 1], F32, name="total")
        nc.scalar.activation(total[:], row_sum[:], ACT.Identity, bias=reserve_sb[:])
        share = keep.tile([P, 1], F32, name="share")
        nc.gpsimd.tensor_tensor(share[:], total[:], minus_one[:], ALU.pow)
        weights = keep.tile([P, PACK, P], F32, name="weights")
        nc.scalar.activation(weights[:], soft[:], ACT.Copy, scale=share[:])
        weights_turned = psum.tile([P, PACK, P], F32, name="weights_turned", tag="bank7")
        for t in range(PACK):
            nc.tensor.transpose(weights_turned[:, t, :], weights[:, t, :], identity[:])
        weights_grouped = keep.tile([P, P, PACK], BF16, name="weights_grouped", align_bytes=64)
        nc.vector.tensor_tensor(
            weights_grouped[:],
            weights_turned[:].rearrange("p t q -> p q t"),
            os_sb[:].unsqueeze(1).to_broadcast([P, P, PACK]),
            ALU.mult,
        )
        weights_q = quantise("weights", weights_grouped[:])

        turned1 = turn(1, ("bank2", "bank3"))
        inverse0 = invert(0, sums0)
        inverse1 = invert(1, group_sums(1))
        scaled1 = scale_values(1, turned1, "grown")

        halves = [(scaled0, inverse0, "bank4", nc.scalar.copy), (scaled1, inverse1, "bank0", nc.vector.tensor_copy)]
        for half, (scaled, inverse, bank, copy_out) in enumerate(halves):
            values_q = normalise("values%d" % half, scaled[:], inverse[:])
            acc = psum.tile([P, HALF], F32, name="acc%d" % half, tag=bank)
            product(acc[:], weights_q, values_q)
            result = keep.tile([P, HALF], F32, name="result%d" % half)
            copy_out(result[:], acc[:])
            nc.sync.dma_start(out[:, half * HALF : (half + 1) * HALF], result[:])
